import numpy as np, ml_dtypes
CORES = [16,18,20,22]
N = 4
BF = ml_dtypes.bfloat16
def gentries(a):
    return np.ascontiguousarray(a.reshape(8, 16, -1).transpose(0, 2, 1)).reshape(8, -1)
def gtable(e):
    e = np.asarray(e); return np.ascontiguousarray(e.reshape(8, -1, 16).transpose(0, 2, 1)).reshape(128, -1).astype(np.int32)
NV, S, TOP, G = 2048, 512, 256, 64
K, K2, LIM, ST, RO = 256, 256, 1024, 416, 4
M = NV - S - TOP; W = NV + (N - 1) * G
FANS = np.array([1, 2, 2, 2, 3, 3, 4, 6, 16])
def twin(d):
    g = np.arange(8)
    return (7 - g, (8 - g) % 8, g)[(d - 1) % 3]
def wire(rng, cut):
    p = np.zeros((16, NV), np.int64)
    for c, im, f in cut:
        b = np.stack([rng.permutation(im) for _ in range(f)])
        p[:, c] = b[rng.permutation(np.concatenate([np.arange(f), rng.integers(0, f, 16 - f)]))]
    return p
def layered(rng, fans):
    pool = np.argsort(np.concatenate([np.arange(NV), rng.integers(0, NV, W - NV)]) + rng.random(W))
    lag = int(rng.choice(np.array([0, 32, 64, 128]))); cut = []
    for a in range(0, NV - S, 128):
        o = S + a + rng.permutation(128); im = rng.permutation(pool[lag + a:lag + a + 128])
        for i in range(0, 128, 32): cut.append((o[i:i + 32], im[i:i + 32], int(rng.choice(fans))))
    rest = rng.permutation(np.concatenate([pool[:lag], pool[lag + NV - S:]])); o = rng.permutation(S)
    for i in range(0, S, 64): cut.append((o[i:i + 64], rest[i:i + 64], int(rng.choice(fans))))
    return wire(rng, cut)
def flat(rng, pool):
    p = np.zeros((16, NV), np.int64)
    for k in range(16):
        o = rng.permutation(pool)[:TOP]; p[k, NV - TOP:] = o
        p[k, :NV - TOP] = rng.permutation(np.setdiff1d(np.arange(W), o))[:NV - TOP]
    return p
def aim(p, k, v, u):
    w = np.nonzero(p[k] == u)[0]
    if len(w): p[k, w[0]] = p[k, v]
    p[k, v] = u
def sweep(rng, miss):
    o = rng.permutation(NV); p = np.zeros((16, NV), np.int64); x = S + int(rng.integers(0, M))
    for k in range(16):
        a = o[k::16]; v = NV - TOP + rng.permutation(TOP - 3)[:len(a)]
        p[k, v] = a; p[k, np.setdiff1d(np.arange(NV), v)] = rng.permutation(np.setdiff1d(np.arange(W), a))[:NV - len(a)]
        if miss: aim(p, k, S, x)
    return p
def back(rng, p, share):
    c = np.full((16, W), NV); np.put_along_axis(c, p, np.broadcast_to(np.arange(NV), (16, NV)), 1); mix = rng.random((16, NV))
    return np.where(mix < share, c[:, :NV], np.where(mix < share + 0.03, rng.integers(0, NV, (16, NV)), NV))
def presence(rng, extra):
    h = np.ones(NV, bool); h[:S] = rng.random(S) > 0.01; h[NV - TOP:] = rng.random(TOP) < 0.2; h[S:NV - TOP] = False
    h[S:NV - TOP] = rng.permutation(M) < LIM + extra - int(np.sum(h))
    return h
def parity(rng):
    return 2 * rng.integers(0, 8, (16, NV)) + rng.integers(0, 2, (1, NV))
def start(rng):
    y = rng.integers(0, 16, (N, 8, 16, NV)); m = rng.integers(0, 2, (N, 8, NV)); b = np.argsort(rng.random((N, 8, NV)), axis=-1)[..., :(N - 1) * G].copy()
    y = np.where(rng.random((N, 8, 1, NV)) < 0.15, 2 * (y >> 1) + rng.integers(0, 2, (N, 8, 1, NV)), y)
    p = np.zeros((N, 8, 16, NV), np.int64); c = p.copy(); h = np.zeros((N, 8, NV), bool)
    for q in range(N):
        for g in range(8):
            p[q, g] = layered(rng, FANS); c[q, g] = back(rng, p[q, g], float(rng.choice(np.array([0.5, 0.8, 0.95]))))
            h[q, g] = presence(rng, int(rng.choice(np.array([-60, 0, 40, 120, K2, 2 * K2]))))
    return y, p, c, m, b, h
def pack(y, p, c, m, b, h):
    y = np.where(h[:, :, None, :], y, -1)
    return {"y0": np.ascontiguousarray(y.reshape(N, 128, NV)).astype(np.float32).astype(BF), "pr": np.ascontiguousarray(p.reshape(N, 128, NV)).astype(np.int32), "co": np.ascontiguousarray(c.reshape(N, 128, NV)).astype(np.int32),
            "mo": np.ascontiguousarray(m).astype(np.int32), "bd": np.stack([gtable(a) for a in b])}
def setup_inputs(rng):
    return pack(*start(rng))
def setup_inputs_spread(rng):
    y, p, c, m, b, h = start(rng)
    y = (rng.random((N, 8, 16, NV)) * rng.choice(np.array([1, 2, 3, 8, 16]), (N, 8, 1, NV))).astype(np.int64); y = np.where(rng.random((N, 8, 1, NV)) < 0.5, 15 - y, y)
    m = (rng.random((N, 8, NV)) < rng.choice(np.array([0.03, 0.5, 0.97]), (N, 8, 1))).astype(np.int64)
    for q in range(N):
        for g in range(1, 8, 2):
            o = rng.permutation(NV); im = rng.permutation(W)[:NV]
            p[q, g] = wire(rng, [(o[i:i + 64], im[i:i + 64], int(rng.choice(np.array([2, 2, 3, 5, 16])))) for i in range(0, NV, 64)])
            c[q, g] = np.where(rng.random((16, NV)) < rng.random((1, NV)) * 0.4, rng.integers(0, NV, (16, NV)), NV)
            h[q, g] = rng.random(NV) < float(rng.choice(np.array([0.1, 0.5, 0.8, 0.95])))
    return pack(y, p, c, m, b, h)
def setup_inputs_ends(rng):
    y, p, c, m, b, h = start(rng)
    kind = rng.integers(0, 5, (N, 8, 1, NV)); one = np.arange(16)[:, None] == rng.integers(0, 16, (N, 8, 1, NV)); rnd = rng.random((N, 8, 16, NV)) < 0.75
    odd = np.where(kind == 0, True, np.where(kind == 1, ~one, np.where(kind == 2, one, rnd)))
    y = np.where(odd, 15, 0); y[:, :, :, 1] = 15; y[:, :, :, 2] = 0
    B = (N - 1) * G // 2; both = np.concatenate([np.arange(B), np.arange(NV - B, NV)])
    for q in range(N):
        for g in range(8):
            pp, hh = p[q, g], h[q, g]; b[q, g] = rng.permutation(both)
            if g == 6: hh[:] = True
            if g == 4:
                hh[:] = True; hh[S:NV - TOP] = rng.permutation(M) < LIM + K2 * RO - 1 - S - TOP
                own = [S + int(v) for v in np.nonzero(hh[S:NV - TOP])[0][:8]]
                for i in range(8):
                    v = own[i]; m[q, g, v] = 1; y[q, g, :, v] = np.where(np.arange(16) <= i, 15, 0)
                    for k in range(16): aim(pp, k, v, v if k == (2 * i + 1) % 16 else 16 + i + 8 * (k % 2))
            if g == 2:
                hh[:] = False; hh[:S] = q % 2 == 0
                if q % 2 == 1: pp[:] = sweep(rng, q % 4 == 3)
            if g not in (2, 4, 6): hh[1] = True; hh[2] = True; hh[NV - 1] = False
            if g % 2 == 1: hh[0] = False; hh[NV - 2] = False; aim(pp, 0, 0, 0); aim(pp, 1, NV - 2, 0)
            for k in range(16): aim(pp, k, NV - 1, 1 + k % 2)
            aim(pp, 15, NV - 3, W - 1)
            z = rng.random((1, NV)); mix = np.where(rng.random((16, NV)) < 0.5, 0, NV)
            c[q, g] = np.where(z < 0.5, NV, np.where(z < 0.75, mix, np.where(z < 0.8, 0, back(rng, pp, 0.95))))
            c[q, g, :, 0] = NV; c[q, g, :, NV - 1] = 0
    return pack(y, p, c, m, b, h)
def setup_inputs_corners(rng):
    y, p, c, m, b, h = start(rng); fixed = np.concatenate([np.arange(S), np.arange(NV - TOP, NV)])
    for q in range(N):
        for g in range(8):
            pp, hh = p[q, g], h[q, g]
            if g < 3:
                dl = (g + q) % 3 - 1; hh[:] = True; m[q, g] = 0
                ta = NV - TOP + 1 + rng.permutation(TOP - 2)[:TOP - 18]; nb = K + dl - (TOP - 17); bs = S + rng.permutation(M)[:nb]; na = len(ta)
                hh[ta] = False; hh[bs] = False; hh[NV - TOP] = False; hh[NV - 1] = False
                for j in range(max(na, nb)): aim(pp, j // min(na, nb), int(ta[j % na]), int(bs[j % nb]))
                for k in range(16):
                    aim(pp, k, NV - TOP, 16 + k); aim(pp, k, NV - 1, NV - TOP if k == 0 else k)
                c[q, g] = back(rng, pp, 0.1); c[q, g, 15] = np.where(rng.random(NV) < 0.5, NV - 1, NV)
            if g == 3:
                y[q, g] = parity(rng); hh[:] = True; hh[S:NV - TOP] = rng.permutation(M) < LIM + K2 * RO - 1 + q % 2 - S - TOP
                c[q, g] = NV; b[q, g] = rng.permutation(fixed)[:(N - 1) * G]
            if g == 4:
                y[q, g] = parity(rng); hh[:] = True; hh[S:NV - TOP] = rng.permutation(M) < LIM + q % 4 - S - TOP
                b[q, g] = rng.permutation(fixed)[:(N - 1) * G]
            if g == 5: hh[:] = False; hh[:S] = q % 2 == 1
            if g == 6:
                for i in range(8): aim(pp, i, NV - 1 - i, NV - 1 - i); hh[NV - 1 - i] = False
                z = rng.integers(0, 4, (1, NV)); last = np.where(np.arange(16)[:, None] == 15, NV - 1, NV)
                c[q, g] = np.where(z == 0, NV - 1, np.where(z == 1, last, np.where(z == 2, np.arange(NV)[None, :], NV)))
            if g == 7:
                p[q, g] = layered(rng, np.array([1, 16])); c[q, g] = back(rng, p[q, g], 0.9); h[q, g] = presence(rng, 0)
    return pack(y, p, c, m, b, h)
def setup_inputs_calm(rng):
    y, p, c, m, b, h = start(rng)
    for q in range(N):
        for g in range(6):
            few = (g + q) % 4; pp, hh = p[q, g], h[q, g]; y[q, g] = parity(rng); hh[:] = True
            for t in range(RO):
                for i in range(few):
                    v = NV - 1 - (4 * t + i); hh[v] = False
                    for k in range(16): aim(pp, k, v, v + 4 if k == 0 and t > 0 else 16 + 4 * t + i + 32 * (k % 2))
            hh[S:NV - TOP] = rng.permutation(M) < LIM - S - (TOP - few * RO)
            c[q, g] = NV; c[q, g, 15] = np.where(rng.random(NV) < 0.3, NV - 1 - 4 * (RO - 1), NV); c[q, g, 0] = np.where(rng.random(NV) < 0.2, NV - 5, NV)
            b[q, g] = rng.permutation(np.concatenate([np.arange(S), np.arange(NV - TOP, NV - 4 * RO)]))[:(N - 1) * G]
        pp, hh = p[q, 6], h[q, 6]; y[q, 6] = parity(rng); u = S + (ST * (RO - 1)) % M; x = NV - RO
        o = np.setdiff1d(np.arange(S, NV - TOP), np.array([u])); hh[:] = True; hh[x:] = False; hh[S:NV - TOP] = False
        hh[rng.permutation(o)[:LIM - S - (TOP - RO)]] = True
        for i in range(RO + 1):
            v = NV - 1 - i if i < RO else u
            for k in range(16):
                a = 16 + i + 32 * (k % 2)
                if k == 0 and 0 < i < RO - 1: a = NV - i
                if k == 0 and i == RO - 1: a = u
                if k == 1 and i == RO - 1: a = NV + 2 * G
                if k == 0 and i == RO: a = NV - RO + 1
                aim(pp, k, v, a)
        c[q, 6] = NV; c[q, 6, 3] = np.where(rng.random(NV) < 0.3, x, NV); c[q, 6, :, u] = NV
        b[q, 6] = rng.permutation(np.concatenate([np.arange(S), np.arange(NV - TOP, x)]))[:(N - 1) * G]; b[q, 6, 2 * G] = u
    return pack(y, p, c, m, b, h)
def setup_inputs_crowd(rng):
    y, p, c, m, b, h = start(rng)
    for q in range(N):
        for g in range(8):
            if g % 4 == 0: p[q, g] = layered(rng, np.array([1]))
            if g % 4 == 1: p[q, g] = layered(rng, np.array([16])); h[q, g] = presence(rng, -60); h[q, g, :S] = True
            if g % 4 > 1:
                h[q, g] = rng.random(NV) < 0.8; h[q, g, :S] = True; h[q, g, NV - TOP:] = False; bs = S + rng.permutation(M)[:2 * TOP]
            if g % 4 == 2:
                p[q, g] = flat(rng, np.arange(S)); h[q, g, bs[:TOP]] = False
                for i in range(TOP): aim(p[q, g], i % 16, NV - TOP + i, int(bs[i]))
            if g % 4 == 3:
                p[q, g] = flat(rng, bs); h[q, g, bs] = False
                for i in range(0, TOP, 2): aim(p[q, g], (i >> 1) % 16, NV - TOP + i, i)
            z = rng.random((1, NV)); last = np.where(np.arange(16)[:, None] == 15, NV - 1, NV)
            c[q, g] = np.where(z < 0.2, NV - 1, np.where(z < 0.4, last, back(rng, p[q, g], 0.6)))
    return pack(y, p, c, m, b, h)
def check_inputs(d):
    bad = []
    for k, lo, hi in (("y0", -1, 15), ("pr", 0, W - 1), ("co", 0, NV), ("mo", 0, 1), ("bd", 0, NV - 1)):
        a = np.asarray(d[k]).astype(np.float64)
        if not (np.min(a) >= lo and np.max(a) <= hi): bad.append("range of " + k)
    y = np.asarray(d["y0"]).astype(np.float32).reshape(N, 8, 16, NV); h = y < 0
    if np.any(y != np.floor(y)): bad.append("whole numbers of y0")
    if np.any(np.any(h, axis=2) != np.all(h, axis=2)): bad.append("absent in all 16 branches or in none, of y0")
    s = np.sort(np.asarray(d["pr"]), axis=2)
    if np.any(s[:, :, 1:] == s[:, :, :-1]): bad.append("different numbers in a row of pr")
    s = np.sort(np.stack([gentries(a) for a in np.asarray(d["bd"])]), axis=2)
    if np.any(s[:, :, 1:] == s[:, :, :-1]): bad.append("different entries of a group of bd")
    return bad
def ghosts(y, bl):
    s = np.zeros((N, 8, 16, (N - 1) * G), np.int64)
    for r in range(N):
        for d in range(1, N):
            q = r ^ d; h = twin(d)
            s[r, :, :, (d - 1) * G:d * G] = np.take_along_axis(y[q][h], bl[q][h, d - 1][:, None, :], 2)
    return s
def reference(y0, pr, co, mo, bd):
    y = y0.astype(np.float32).astype(np.int64).reshape(N, 8, 16, NV); ph = np.zeros((N, 8, 16, NV), np.int64)
    p = pr.astype(np.int64).reshape(N, 8, 16, NV); c = co.astype(np.int64).reshape(N, 8, 16, NV); m = mo.astype(np.int64)
    bl = np.stack([gentries(a) for a in bd]).astype(np.int64).reshape(N, 8, N - 1, G)
    want = (y[:, :, 0] < 0) & (np.arange(NV) >= NV - TOP)
    for t in range(RO):
        gh = ghosts(y, bl); a = np.concatenate([y, gh], axis=3)
        tl = np.argsort(~want, axis=2, kind="stable")[..., :K]; live = np.take_along_axis(want, tl, 2)
        pt = np.take_along_axis(p, tl[:, :, None, :], 3)
        v = np.take_along_axis(a, pt.reshape(N, 8, 1, 16 * K), 3).reshape(N, 8, 16, 16, K)
        gone = v[:, :, 0] < 0; diff = np.max(v, axis=3) - np.min(v, axis=3); named = np.zeros((N, 8, W), bool)
        i, j, k, s = np.nonzero(gone & live[:, :, None, :]); named[i, j, pt[i, j, k, s]] = True
        i, j, s = np.nonzero(live & ~np.any(gone, axis=2)); u = tl[i, j, s]
        y[i, j, :, u] = diff[i, j, :, s]; ph[i, j, :, u] = 0
        want = want | named[:, :, :NV]; want[i, j, u] = False
        here = y[:, :, 0] >= 0; e = np.clip(np.add.reduce(here.astype(np.int64), axis=2) - LIM, 0, K2)
        ring = S + (np.arange(M) + ST * t) % M
        rl = ring[np.argsort(~here[:, :, ring], axis=2, kind="stable")[..., :K2]]; live = np.take_along_axis(here, rl, 2)
        wx = np.concatenate([want, np.zeros((N, 8, 1), bool)], axis=2)
        ct = np.take_along_axis(c, rl[:, :, None, :], 3).reshape(N, 8, 16 * K2)
        held = np.any(np.take_along_axis(wx, ct, 2).reshape(N, 8, 16, K2), axis=2)
        fr = (live & ~held).astype(np.int64); go = (fr == 1) & (np.add.accumulate(fr, axis=2) - fr < e[:, :, None])
        has = np.concatenate([here, gh[:, :, 0] >= 0], axis=2); pt = np.take_along_axis(p, rl[:, :, None, :], 3).reshape(N, 8, 16 * K2)
        dirty = ~np.all(np.take_along_axis(has, pt, 2).reshape(N, 8, 16, K2), axis=2)
        old = np.take_along_axis(y, rl[:, :, None, :], 3)
        f = np.where(dirty[:, :, None, :], (old & 1) * np.take_along_axis(m, rl, 2)[:, :, None, :], 0); cnt = np.add.reduce(f, axis=2)
        i, j, s = np.nonzero(go); u = rl[i, j, s]
        ph[i, j, :, u] = f[i, j, :, s]; y[i, j, :, u] = -1
        want[i, j, u] = (cnt[i, j, s] >= 1) & (cnt[i, j, s] <= 15)
        lost = y[:, :, 0] < 0
        for r in range(N):
            for d in range(1, N):
                q = r ^ d; h = twin(d)[:, None]; ix = bl[q][twin(d), d - 1]
                want[q, h, ix] = want[q, h, ix] | (named[r, :, NV + (d - 1) * G:NV + d * G] & lost[q][h, ix])
    return {"yy": y.reshape(N, 128, NV).astype(np.float32).astype(BF), "yf": ph.reshape(N, 128, NV).astype(np.float32).astype(BF), "yw": want.astype(np.float32).astype(BF)}

@@ -1,0 +1,469 @@
+import numpy as np
+from concourse.bass import DstId, RemoteDMATransfer
+from concourse.mybir import AluOpType, ActivationFunctionType
+
+N = 4
+WW = 2752
+VG, VD, HV = 1, 1, 2
+NS, S0, S1, S2 = 10, 2, 3, 4
+NS0, SE = 12, 4
+B16, F32, I32, U16 = "bfloat16", "float32", "int32", "uint16"
+SB = {
+    "yv": (WW, B16), "wn": (WW, B16), "mk": (WW, F32), "prw": (WW, I32), "cow": (2240, I32), "mob": (2240, B16),
+    "moi": (80, I32), "mof": (80, B16), "bdi": (12, I32), "bdu": (12, U16),
+    "sw": (3984, F32), "mx": (1024, B16), "mn": (1024, B16), "c8": (256, F32),
+    "vb": (4096, B16), "smx": (4096, B16), "smn": (4096, B16), "dg": (4096, B16),
+    "hv": (4096, B16), "hm": (3072, B16),
+    "oy": (2048, B16), "of": (2048, B16), "ow": (2048, B16),
+    "sg": (768, B16), "lg": (768, B16), "sn": (768, B16), "ln": (768, B16),
+    "pc": (8, I32), "fc0": (16, F32), "pm": (128, F32), "qm": (128, F32), "mg": (128, F32), "ki": (16, F32),
+    "idm": (128, B16), "nid": (128, B16), "one": (128, B16), "tri": (128, B16), "trt": (128, B16),
+    "pe1": (128, B16), "pe2": (128, B16), "bsel": (144, B16),
+    "t16": (16, B16), "qt": (16, B16), "c16": (16, B16), "sl": (16, U16), "pt1": (128, B16), "pt2": (40, B16),
+    "o256": (256, B16), "fb": (288, B16), "fc": (192, B16), "dv": (144, F32), "tc": (16, F32), "tb": (16, F32),
+    "off": (10, U16), "ff": (256, B16), "tl": (18, U16), "rl": (16, U16), "w1": (16, F32), "w2": (16, F32),
+    "gp": (272, F32), "tt": (512, F32), "ptt": (256, U16), "pd": (256, U16), "pu": (256, U16), "cu": (256, U16),
+    "otl": (256, B16), "rr": (256, B16), "yn": (256, B16), "sgn": (128, B16), "junk": (128, B16), "ec": (1, F32),
+    "ebc": (256, B16), "orl": (256, B16), "pa": (256, B16),
+    "mog": (256, B16), "fs": (256, B16), "am": (256, B16), "gy": (192, B16), "ga": (192, B16), "nw": (256, B16),
+    "fr": (256, B16), "cm": (258, B16), "go": (256, B16), "m1": (256, B16), "nt": (192, B16), "nu": (192, B16),
+    "m0": (256, B16),
+}
+SCRATCH = {k: ("sbuf", [128, v[0]], v[1]) for k, v in SB.items()}
+for _i in range(8):
+    SCRATCH["ps%d" % _i] = ("psum", [128, 512], F32)
+NDMA = 16
+SEMAPHORES = ["qv", "qs", "qp", "qg", "sent"] + ["d%d" % i for i in range(NDMA)] + ["a%d" % i for i in range(8)]
+
+
+def rank_program(g, core, T, topo):
+    rank = T.rank_of(core)
+    if rank is None:
+        return
+    A = AluOpType
+    F = ActivationFunctionType
+    Q = {"v": g.vector, "s": g.scalar, "p": g.tensor, "g": g, "y": g.sync}
+    ops = []
+    nd = [0]
+
+    def R(name, a=None, b=None, s=None, part=None):
+        t = T[name]
+        m = np.zeros(t.shape[1], bool)
+        sl = slice(a, b, s)
+        m[sl] = True
+        if name.startswith("ps"):
+            m[:] = True
+        ap = t[:, sl] if part is None else t[part, sl]
+        return (ap, [(name, m)])
+
+    def IND(win, off):
+        return (win[0].indirect(off[0]), win[1], off[1])
+
+    def acc(xs):
+        out = []
+        for x in xs:
+            if isinstance(x, tuple):
+                out += x[1]
+                if len(x) == 3:
+                    out += x[2]
+        return out
+
+    def ap(x):
+        return x[0] if isinstance(x, tuple) else x
+
+    def put(q, emit, ins, out):
+        rd = acc(ins)
+        wr = []
+        for o in out:
+            wr += o[1]
+            if len(o) == 3:
+                rd += o[2]
+        ops.append((q, emit, rd, wr, None, 0))
+
+    def cp(o, i):
+        put("v", lambda: g.vector.tensor_copy(o[0], i[0]), [i], [o])
+
+    def tt(o, a, b, op):
+        put("v", lambda: g.vector.tensor_tensor(o[0], a[0], b[0], op), [a, b], [o])
+
+    def ts(o, a, s1, op0, s2=None, op1=None):
+        if op1 is None:
+            put("v", lambda: g.vector.tensor_scalar(o[0], a[0], ap(s1), None, op0), [a, s1], [o])
+        else:
+            put("v", lambda: g.vector.tensor_scalar(o[0], a[0], ap(s1), ap(s2), op0, op1), [a, s1, s2], [o])
+
+    def scan(o, d0, d1, op0, op1):
+        put("v", lambda: g.vector.tensor_tensor_scan(o[0], d0[0], d1[0], 0.0, op0, op1), [d0, d1], [o])
+
+    def ms(o, c):
+        put("v", lambda: g.vector.memset(o[0], c), [], [o])
+
+    def tr(o, i):
+        put("v", lambda: g.vector.transpose(o[0], i[0]), [i], [o])
+
+    def act(o, i, f, scale=1.0, bias=0.0, accum=None):
+        if len(o) == 3:
+            put("s", lambda: g.scalar.activation(o[0], i[0], f), [i], [o])
+        elif accum is None:
+            put("s", lambda: g.scalar.activation(o[0], i[0], f, bias=bias, scale=ap(scale)), [i, scale], [o])
+        else:
+            put("s", lambda: g.scalar.activation(o[0], i[0], f, bias=bias, scale=scale, accum_out=accum[0]),
+                [i], [o, accum])
+
+    def mm(terms):
+        def emit():
+            h = None
+            for n, (o, l, r) in enumerate(terms):
+                h = g.tensor.matmul(o[0], l[0], r[0], n == 0, n == len(terms) - 1)
+            return h
+        put("p", emit, [x[1] for x in terms] + [x[2] for x in terms], [terms[0][0]])
+
+    def iota(o, pat, base, cm_, flt):
+        if flt:
+            put("g", lambda: g.iota(o[0], pat, base, cm_, allow_small_or_imprecise_dtypes=True), [], [o])
+        else:
+            put("g", lambda: g.iota(o[0], pat, base, cm_), [], [o])
+
+    def dma(q, o, i, after=()):
+        s = "d%d" % nd[0]
+        nd[0] += 1
+        ops.append((q, lambda: Q[q].dma_start(ap(o), ap(i)), acc([i]) + acc(after), acc([o]), s, 16))
+
+    nsent = [0]
+
+    def exchange(src, dst, slot, sem):
+        trs = []
+        tot = 0
+        for d in range(1, N):
+            peer = T.cores[rank ^ d]
+            rid, pid, _ = topo.addr(peer)
+            eng = topo.engines(core, peer)
+            per = len(eng) // N
+            mask = sum(1 << e for e in eng[per * (d - 1):per * d])
+            tot += len(topo.engines(peer, core)) // N
+            nsent[0] += per
+            a = 192 * slot + 64 * (d - 1)
+            trs.append(RemoteDMATransfer(dst_ids=[DstId(rid=rid, pnc=pid)], dma_engine_mask=mask,
+                                         remote_sem=T.sem[sem], src=T[src][:, a:a + 64], dst=T[dst][:, a:a + 64]))
+        ops.append(("g", lambda: g.remote_dma_fused(trs, local_sem=T.sem.sent),
+                    acc([R(src, 192 * slot, 192 * slot + 192)]), [], "-", 0))
+        ops.append(("x", None, [], acc([R(dst, 192 * slot, 192 * slot + 192)]), sem, tot))
+
+    def sel(x):
+        return R("bsel", 15 - x, 143 - x)
+
+    def wrap(out, name, a, b, more=()):
+        mm([(out, sel(x), R(name, a + x, b, 16)) for x in range(16)] + list(more))
+
+    def turn(ps, name, slot):
+        for d, m in enumerate(("pe1", "pe2", "idm")):
+            a = 192 * slot + 64 * d
+            mm([(R(ps, 64 * d, 64 * d + 64), R(m), R(name, a, a + 64))])
+
+    def pc(i):
+        return R("pc", i, i + 1)
+
+    def fcol(i):
+        return R("fc0", i, i + 1)
+
+    dma("y", R("wn", 1792, 2048), T.y0[:, 1792:2048])
+    dma("y", R("yv", 0, 2048), T.y0[:])
+    dma("s", R("prw", 1792, 2048), T.pr[:, 1792:2048])
+    dma("s", R("bdi"), T.bd[:])
+    dma("y", R("moi"), T.mo[:, 512:1792])
+    iota(pc(0), [[0, 1]], 0, 1, False)
+    iota(R("ki"), [[1, 16]], 0, 0, True)
+    iota(R("pm"), [[-1, 128]], 0, 1, True)
+    iota(R("prw", 2048, WW), [[1, WW - 2048]], 2048, 0, False)
+    iota(R("qm"), [[16, 8], [-1, 16]], -112, 1, True)
+    iota(R("mg"), [[1, 8], [0, 16]], 0, 0, True)
+    iota(R("pt1"), [[32, 128]], 4096, 0, True)
+    iota(R("pt2"), [[64, 40]], 8192, 0, True)
+    iota(R("sw", 1536, 1792), [[0, 256]], 0, 0, True)
+    ms(R("mx"), 1.0)
+    for a in range(0, WW, 1024):
+        act(R("mk", a, min(a + 1024, WW)), R("mx", 0, min(1024, WW - a)), F.Copy)
+    act(R("mn"), R("mx"), F.Copy, scale=0.0)
+    ms(R("bsel"), 0.0)
+    ts(pc(1), pc(0), 4, A.arith_shift_right)
+    ts(pc(2), pc(0), 15, A.bitwise_and)
+    ms(R("c8"), 8.0)
+    tt(pc(3), pc(0), pc(1), A.add)
+    cp(fcol(0), pc(1))
+    cp(fcol(1), pc(2))
+    ts(pc(4), pc(3), 1, A.bitwise_and)
+    ts(R("idm"), R("pm"), 0.0, A.is_equal)
+    ts(R("bsel", 15, 143, 16), R("ki", 0, 8), fcol(0), A.is_equal)
+    ts(fcol(3), fcol(1), 0.0, A.is_equal, 256.0, A.mult)
+    cp(fcol(2), pc(4))
+    ts(R("t16"), R("ki"), 16.0, A.mult)
+    ts(fcol(6), fcol(1), 448.0, A.add)
+    ts(R("m0"), R("wn", 1792, 2048), 0.0, A.min, 28.0, A.mult)
+    wrap(R("ps1", 0, 16), "m0", 0, 256, [(R("ps1", 0, 16), R("idm"), R("t16"))])
+    ts(fcol(4), fcol(3), 240.0, A.add, fcol(2), A.mult)
+    cp(R("bdu"), R("bdi"))
+    ts(fcol(5), fcol(1), 16.0, A.mult, fcol(4), A.add)
+    ms(R("yv", 2240, WW), 0.0)
+    ts(R("sl"), R("ki"), fcol(5), A.add)
+    ms(R("wn", 2240, WW), 0.0)
+    act(R("sg", 0, 192), IND(R("yv", 0, 2048), R("bdu")), F.Relu, bias=1.0)
+    exchange("sg", "lg", 0, "a0")
+    ts(R("tl", 0, 16), R("ps1", 0, 16), fcol(6), A.add)
+    ts(R("tl", 16, 17), R("ps1", 0, 1), fcol(6), A.add)
+    iota(R("mob"), [[0, 2240]], 0, 0, True)
+    for name, a, b, v in (("c16", 0, 16, 16), ("o256", 0, 256, 1), ("fb", 0, 2, 0), ("fb", 272, 288, 1),
+                          ("fc", 0, 2, 0), ("fc", 176, 192, 1), ("cm", 0, 2, 0)):
+        iota(R(name, a, b), [[0, b - a]], v, 0, True)
+    iota(R("cow", 1280, 2240), [[0, 960]], 2048, 0, False)
+    iota(R("sw", 0, 1536), [[0, 1536]], 0, 0, True)
+    dma("y", R("prw", 0, 1792), T.pr[:, 0:1792], after=[R("lg", 0, 192)])
+    dma("y", R("cow", 0, 1280), T.co[:, 512:1792])
+
+    def later_constants():
+        ts(R("pe1"), R("qm"), 0.0, A.is_equal)
+        ts(R("pe2", 16, 128), R("qm", 16, 128), 16.0, A.is_equal)
+        ts(R("pe2", 0, 16), R("pm", 0, 16), 0.0, A.is_equal)
+        ts(R("wn", 0, 1792), R("yv", 0, 1792), 0.25, A.mult)
+        ms(R("mx", 0, 1024, 16), 0.0)
+        cp(R("mof"), R("moi"))
+        ts(R("nid"), R("pm"), 0.0, A.is_equal, -1.0, A.mult)
+        ms(R("mn", 0, 1024, 16), 1e20)
+        ts(R("qt"), R("ki"), -1.0 / 256, A.mult)
+        ts(R("trt"), R("pm"), 0.0, A.is_le)
+        ts(R("one"), R("mg"), fcol(0), A.is_equal)
+        ts(fcol(7), fcol(1), 2304.0, A.add)
+        tt(R("tri"), R("one"), R("trt"), A.mult)
+        dma("y", R("mob", 0, 1280, part=slice(0, 128, 16)), R("mof"))
+
+    def cells_a(fb, n, spare, high):
+        r = n - 16
+        t = [(R("ps2", 0, n), R("tri"), R(fb, n, 2 * n)), (R("ps2", 0, r), R("nid"), R("pt1", 0, r)),
+             (R("ps2", r, n), R("nid"), spare)]
+        if high:
+            t.append((R("ps2", r, n), R("nid"), R("c16")))
+        scan(R(fb, 1, n), R(fb, n, 2 * n - 1), R(fb, n, 2 * n - 1), A.add, A.max)
+        mm(t)
+        act(R("dv", 0, n), R("ps2", 0, n), F.Identity, scale=-1.0, bias=16.5)
+        q = n // 16
+        wrap(R("ps1", 0, 2 * q), fb, 0, 2 * n, [(R("ps1", q, 2 * q), R("idm"), R("qt", 0, q))])
+
+    def cells_b(n, use):
+        q = n // 16
+        a = 256 * (6 - use)
+        ts(R("tc", 0, q), R("ps1", q, 2 * q), -4096.0, A.mult, fcol(7), A.add)
+        tt(R("tb", 0, q), R("ps1", 0, q), R("tc", 0, q), A.max)
+        cp(R("off", 0, q), R("tb", 0, q))
+        cp(IND(R("sw", a, a + 2448), R("off", 0, q)), R("dv", 0, n))
+        scan(R("ff"), R("o256"), R("sw", a, a + 256), A.add, A.max)
+        wrap(R("ps1", 0, 16), "ff", 0, 256)
+
+    left = {"v": [], "s": []}
+
+    def rows(nv, ns):
+        for _ in range(min(nv, len(left["v"]))):
+            k = left["v"].pop(0)
+            cp(IND(R("wn"), R("ptt", 16 * k, 16 * k + 16)), R("vb", k, 4096, 16))
+        for _ in range(min(ns, len(left["s"]))):
+            k = left["s"].pop(0)
+            act(IND(R("mk"), R("ptt", 16 * k, 16 * k + 16)), R("c8"), F.Silu)
+
+    def release_values(t):
+        tt(R("m1"), R("go"), R("am"), A.mult)
+        tt(IND(R("yv", 512, WW), R("rl")), R("orl"), R("m1"), A.add)
+
+    for t in range(4):
+        lo = 1792 if t == 0 else 0
+        tl = R("tl", 0, 16)
+        ns = NS0 if t == 0 else NS
+        left["v"] = list(range(16 - ns))
+        left["s"] = list(range(16 - ns, 16))
+        if t > 0:
+            wrap(R("ps0", 0, 128), "wn", 0, 2048)
+            release_values(t - 1)
+            ts(R("fb", 144, 272), R("ps0", 0, 128), -8.0, A.is_lt)
+            cells_a("fb", 144, R("pt2", 6, 22), True)
+            cells_b(144, 2 * t - 1)
+            ts(R("tl", 0, 16), R("ps1", 0, 16), 1.0 / 32, A.mult, -2048.0, A.add)
+            ts(R("tl", 16, 17), R("ps1", 0, 1), 1.0 / 32, A.mult, -2048.0, A.add)
+            cp(R("pd"), IND(R("prw", lo, WW), tl))
+            turn("ps6", "lg", t)
+            act(R("yv", 2048, 2240), R("ps6", 0, 192), F.Identity, bias=-1.0)
+        cp(R("gp"), IND(R("prw", lo, WW), R("tl", 0, 17)))
+        tr(R("tt", 0, 256), R("gp", 0, 256))
+        tr(R("tt", 256, 512), R("gp", 16, 272))
+        cp(R("ptt"), IND(R("tt"), R("sl")))
+        if t == 0:
+            rows(0, SE)
+            cp(R("pd"), R("gp", 0, 256))
+            later_constants()
+            turn("ps6", "lg", t)
+            act(R("yv", 2048, 2240), R("ps6", 0, 192), F.Identity, bias=-1.0)
+        act(R("wn", 2048, 2240), R("ps6", 0, 192), F.Identity, scale=0.25, bias=-0.25)
+        for c in range(4):
+            a = 1024 * c
+            if c < VG:
+                cp(R("vb", a, a + 1024), IND(R("yv"), R("pd", 64 * c, 64 * c + 64)))
+            else:
+                act(R("vb", a, a + 1024), IND(R("yv"), R("pd", 64 * c, 64 * c + 64)), F.Copy)
+            scan(R("smn", a, a + 1024), R("mn", 0, 1024), R("vb", a, a + 1024), A.add, A.min)
+            if c == 3:
+                act(R("otl"), IND(R("yv", lo, WW), tl), F.Copy)
+                rows(0, S0)
+                act(R("rr"), R("smn", 15, 4096, 16), F.Relu, scale=-64.0)
+            scan(R("smx", a, a + 1024), R("mx"), R("vb", a, a + 1024), A.mult, A.max)
+        p3 = R("ps3", 0, 256)
+        mm([(p3, R("nid"), R("smn", 15, 4096, 16)), (p3, R("nid"), R("otl")), (p3, R("nid"), R("rr")),
+            (p3, R("idm"), R("smx", 15, 4096, 16))])
+        act(R("yn"), p3, F.Relu)
+        rows(1, 0)
+        tt(IND(R("yv", lo, WW), tl), R("yn"), R("otl"), A.add)
+        wrap(R("ps0", 0, 128), "yv", 0, 2048)
+        rows(2, S1)
+        c0 = 26 * t
+        ts(R("fc", 96, 176 - c0), R("ps0", 32 + c0, 112), 0.0, A.is_ge)
+        if c0:
+            ts(R("fc", 176 - c0, 176), R("ps0", 32, 32 + c0), 0.0, A.is_ge)
+        spare = (R("pt1", 108, 124), R("pt2", 17, 33), R("pt2", 4, 20), R("pt1", 110, 126))[t]
+        cells_a("fc", 96, spare, t in (1, 2))
+        act(R("sgn"), R("ps0", 0, 128), F.Sign, bias=0.5)
+        rows(1, S2)
+        cells_b(96, 2 * t)
+        mm([(R("ps7", 0, 128), R("one"), R("sgn"))])
+        rows(1, 0)
+        if t == 0:
+            ts(R("rl"), R("ps1", 0, 16), 1.0 / 32, A.mult, -2048.0, A.add)
+        else:
+            ts(R("w1"), R("ps1", 0, 16), 32.0 * (2048 + 1280 - 416 * t), A.is_ge, -32.0 * 1280, A.mult)
+            tt(R("w2"), R("ps1", 0, 16), R("w1"), A.add)
+            ts(R("rl"), R("w2"), 1.0 / 32, A.mult, 416.0 * t - 2048.0, A.add)
+        rl = R("rl")
+        cp(R("pu"), IND(R("prw", 512, WW), rl))
+        rows(0, 16)
+        act(R("junk"), R("ps7", 0, 128), F.Identity, scale=2.0, accum=R("ec"))
+        act(R("ebc"), R("o256"), F.Relu, scale=R("ec"))
+        act(R("orl"), IND(R("yv", 512, WW), rl), F.Copy)
+        act(R("mog"), IND(R("mob"), rl), F.Copy)
+        act(R("pa"), R("orl"), F.Identity, bias=256.5)
+        cp(R("cu"), IND(R("cow"), rl))
+        for c in range(4):
+            a = 1024 * c
+            lst = IND(R("yv"), R("pu", 64 * c, 64 * c + 64))
+            if c >= 4 - VD:
+                rows(16, 0)
+                ts(R("dg", a, a + 1024), lst, 0.0, A.min, -1.0 / 64, A.mult)
+            else:
+                act(R("dg", a, a + 1024), lst, F.Relu, scale=-1.0 / 64)
+            o = R("ps4", 64 * c, 64 * c + 64)
+            mm([(o, R("idm"), R("dg", a + k, a + 1024, 16)) for k in range(16)]
+               + [(o, R(m), R(x, 64 * c, 64 * c + 64)) for m, x in (("one", "mog"), ("idm", "pa"), ("nid", "orl"))])
+        rows(16, 0)
+        tt(R("wn", 0, 2240), R("wn", 0, 2240), R("mk", 0, 2240), A.mult)
+        ts(R("sn", 192 * t, 192 * t + 192), R("wn", 2048, 2240), -0.5, A.is_lt, 7.0, A.mult)
+        exchange("sn", "ln", t, "a%d" % (4 + t))
+        if t < 3:
+            iota(R("mk", 0, 2240), [[0, 2240]], 1, 0, True)
+        ms(R("wn", 2048, 2240), 0.0)
+        tt(IND(R("wn", lo, WW), tl), R("yn"), R("otl"), A.add)
+        for c in range(4):
+            a = 1024 * c
+            lst = IND(R("wn", 0, 2064), R("cu", 64 * c, 64 * c + 64))
+            if c < HV:
+                cp(R("hv", a, a + 1024), lst)
+                scan(R("hm", a, a + 1024), R("mn"), R("hv", a, a + 1024), A.add, A.min)
+                continue
+            act(R("hv", a, a + 1024), lst, F.Relu, scale=-1.0, bias=-0.5)
+            if c == HV:
+                act(R("fs"), R("ps4", 0, 256), F.Sign, bias=-258.0 - 1.0 / 128)
+            o = R("ps5", 64 * c, 64 * c + 64)
+            mm([(o, R("idm"), R("hv", a + k, a + 1024, 16)) for k in range(16)])
+            if c == HV:
+                mm([(p3, R("one"), R("fs"))])
+        act(R("nw"), p3, F.Square, scale=3.75 ** 0.5 / 16)
+        act(R("fr", 64 * HV, 256), R("ps5", 64 * HV, 256), F.Relu, scale=-8.0, bias=4.0)
+        p4 = R("ps4", 0, 256)
+        mm([(p4, R("idm"), R("orl")), (p4, R("idm"), R("orl")), (p4, R("idm"), R("fs"))])
+        turn("ps7", "ln", t)
+        if t < 3:
+            act(R("gy"), IND(R("yv", 0, 2048), R("bdu")), F.Copy)
+        act(R("am"), p4, F.Identity, scale=0.125, bias=0.375)
+        act(R("nt"), R("ps7", 0, 192), F.Identity, bias=1.0)
+        ts(R("fr", 0, 64 * HV), R("hm", 15, 1024 * HV, 16), -0.5, A.is_ge, 4.0, A.mult)
+        scan(R("cm", 2, 258), R("fr"), R("ebc"), A.add, A.min)
+        tt(R("go"), R("cm", 1, 257), R("cm", 2, 258), A.subtract)
+        if t == 3:
+            release_values(t)
+            for h in range(2):
+                a = 1024 * h
+                ts(R("oy", a, a + 1024), R("yv", a, a + 1024), -1.0, A.max)
+                dma("y", T.yy[:, a:a + 1024], R("oy", a, a + 1024))
+                act(R("of", a, a + 1024), R("yv", a, a + 1024), F.Relu, scale=-1.0, bias=-1.0)
+                dma("s", T.yf[:, a:a + 1024], R("of", a, a + 1024))
+        tt(IND(R("wn", 512, WW), rl), R("go"), R("nw"), A.add)
+        if t < 3:
+            act(R("ga"), IND(R("wn", 0, 2048), R("bdu")), F.Relu, scale=-128.0)
+            p6 = R("ps6", 0, 192)
+            mm([(p6, R("idm"), R("gy")), (p6, R("nid"), R("ga"))])
+            act(R("sg", 192 * t + 192, 192 * t + 384), p6, F.Relu, bias=1.0)
+            exchange("sg", "lg", t + 1, "a%d" % (t + 1))
+        tt(R("nu"), IND(R("wn", 0, 2048), R("bdu")), R("nt"), A.mult)
+        cp(IND(R("wn", 0, 2048), R("bdu")), R("nu"))
+    ts(R("ow"), R("wn", 0, 2048), -0.5, A.is_lt)
+    dma("y", T.yw[:], R("ow", part=slice(0, 128, 16)))
+
+    hist = {}
+    deps = []
+    for n, (q, emit, rd, wr, sem, cnt) in enumerate(ops):
+        d = set()
+        for kind, lst in ((0, rd), (1, wr)):
+            for name, m in lst:
+                bank = name.startswith("ps")
+                for (j, mj, kj) in hist.get(name, []):
+                    if j == n or not (kind or kj or bank) or not (m & mj).any():
+                        continue
+                    if ops[j][0] == q and ops[j][4] is None and sem is None and (q == "p" or not (kind or kj)):
+                        continue
+                    d.add(j)
+        for kind, lst in ((0, rd), (1, wr)):
+            for name, m in lst:
+                hist.setdefault(name, []).append((n, m, kind))
+        last = {}
+        for j in d:
+            key = ops[j][4] or ops[j][0]
+            last[key] = max(last.get(key, -1), j)
+        deps.append(last)
+    seen = {q: {} for q in Q}
+    need = []
+    marked = set()
+    for n, op in enumerate(ops):
+        w = []
+        if op[0] != "x":
+            for key, j in deps[n].items():
+                if seen[op[0]].get(key, -1) < j:
+                    seen[op[0]][key] = j
+                    w.append(j)
+                    marked.add(j)
+        need.append(w)
+    count = {q: 0 for q in Q}
+    val = {}
+    for n, (q, emit, rd, wr, sem, cnt) in enumerate(ops):
+        if sem is None:
+            if n in marked:
+                count[q] += 1
+                val[n] = ("q" + q, count[q])
+        else:
+            val[n] = (sem, cnt)
+    for n, (q, emit, rd, wr, sem, cnt) in enumerate(ops):
+        if q == "x":
+            continue
+        for j in need[n]:
+            Q[q].wait_ge(T.sem[val[j][0]], val[j][1])
+        h = emit()
+        if sem is None:
+            if n in marked:
+                h.then_inc(T.sem["q" + q], 1)
+        elif sem != "-":
+            h.then_inc(T.sem[sem], 16)
+    for n, op in enumerate(ops):
+        if op[4] not in (None, "-") and n not in marked:
+            g.sync.wait_ge(T.sem[op[4]], op[5])
+    g.wait_ge(T.sem.sent, nsent[0])

@@ -5,13 +5,14 @@ from concourse.mybir import AluOpType, ActivationFunctionType
 N = 4
 WW = 2752
 VG, VD, HV = 1, 1, 2
-NS, S0, S1, S2 = 10, 2, 3, 4
-NS0, SE = 12, 4
+NS, S0, S1, S2 = 10, 1, 3, 4
+MB = 2
+NS0, SE = 10, 1
 B16, F32, I32, U16 = "bfloat16", "float32", "int32", "uint16"
 SB = {
     "yv": (WW, B16), "wn": (WW, B16), "mk": (WW, F32), "prw": (WW, I32), "cow": (2240, I32), "mob": (2240, B16),
     "moi": (80, I32), "mof": (80, B16), "bdi": (12, I32), "bdu": (12, U16),
-    "sw": (3984, F32), "mx": (1024, B16), "mn": (1024, B16), "c8": (256, F32),
+    "sw": (3984, F32), "mx": (1024, B16), "mn": (1024, B16), "c8": (256, F32), "id32": (128, F32),
     "vb": (4096, B16), "smx": (4096, B16), "smn": (4096, B16), "dg": (4096, B16),
     "hv": (4096, B16), "hm": (3072, B16),
     "oy": (2048, B16), "of": (2048, B16), "ow": (2048, B16),
@@ -124,6 +125,9 @@ def rank_program(g, core, T, topo):
         else:
             put("g", lambda: g.iota(o[0], pat, base, cm_), [], [o])
 
+    def asel(o, i, pat, op, base, cm_):
+        put("g", lambda: g.affine_select(o[0], i[0], pat, op, 0.0, base, cm_), [i], [o])
+
     def dma(q, o, i, after=()):
         s = "d%d" % nd[0]
         nd[0] += 1
@@ -175,15 +179,12 @@ def rank_program(g, core, T, topo):
     iota(R("ki"), [[1, 16]], 0, 0, True)
     iota(R("pm"), [[-1, 128]], 0, 1, True)
     iota(R("prw", 2048, WW), [[1, WW - 2048]], 2048, 0, False)
-    iota(R("qm"), [[16, 8], [-1, 16]], -112, 1, True)
-    iota(R("mg"), [[1, 8], [0, 16]], 0, 0, True)
-    iota(R("pt1"), [[32, 128]], 4096, 0, True)
-    iota(R("pt2"), [[64, 40]], 8192, 0, True)
-    iota(R("sw", 1536, 1792), [[0, 256]], 0, 0, True)
     ms(R("mx"), 1.0)
+    asel(R("pe1"), R("mx", 0, 128), [[16, 8], [-1, 16]], A.is_equal, -112, 1)
+    asel(R("pe2", 16, 128), R("mx", 0, 112), [[16, 7], [-1, 16]], A.is_equal, -112, 1)
+    asel(R("pe2", 0, 16), R("mx", 0, 16), [[-1, 16]], A.is_equal, 0, 1)
     for a in range(0, WW, 1024):
         act(R("mk", a, min(a + 1024, WW)), R("mx", 0, min(1024, WW - a)), F.Copy)
-    act(R("mn"), R("mx"), F.Copy, scale=0.0)
     ms(R("bsel"), 0.0)
     ts(pc(1), pc(0), 4, A.arith_shift_right)
     ts(pc(2), pc(0), 15, A.bitwise_and)
@@ -205,14 +206,27 @@ def rank_program(g, core, T, topo):
     ts(fcol(5), fcol(1), 16.0, A.mult, fcol(4), A.add)
     ms(R("yv", 2240, WW), 0.0)
     ts(R("sl"), R("ki"), fcol(5), A.add)
-    ms(R("wn", 2240, WW), 0.0)
     act(R("sg", 0, 192), IND(R("yv", 0, 2048), R("bdu")), F.Relu, bias=1.0)
     exchange("sg", "lg", 0, "a0")
+    act(R("mn"), R("mx"), F.Copy, scale=0.0)
+    iota(R("wn", 2240, WW), [[0, WW - 2240]], 0, 0, True)
+    iota(R("nid"), [[0, 128]], -1, 0, True)
+    asel(R("nid"), R("nid"), [[-1, 128]], A.is_equal, 0, 1)
+    iota(R("one"), [[0, 128]], 1, 0, True)
+    asel(R("one"), R("one"), [[-16, 8], [0, 16]], A.is_ge, 0, 1)
+    asel(R("one"), R("one"), [[16, 8], [0, 16]], A.is_ge, 15, -1)
+    asel(R("tri"), R("one"), [[1, 128]], A.is_ge, 0, -1)
+    iota(R("id32"), [[0, 128]], 1, 0, True)
+    asel(R("id32"), R("id32"), [[-1, 128]], A.is_equal, 0, 1)
+    iota(R("pt1"), [[32, 128]], 4096, 0, True)
+    iota(R("pt2"), [[64, 40]], 8192, 0, True)
+    iota(R("sw", 1536, 1792), [[0, 256]], 0, 0, True)
     ts(R("tl", 0, 16), R("ps1", 0, 16), fcol(6), A.add)
     ts(R("tl", 16, 17), R("ps1", 0, 1), fcol(6), A.add)
+    for name, a, b, v in (("fc", 0, 2, 0), ("fc", 176, 192, 1), ("o256", 0, 256, 1)):
+        iota(R(name, a, b), [[0, b - a]], v, 0, True)
     iota(R("mob"), [[0, 2240]], 0, 0, True)
-    for name, a, b, v in (("c16", 0, 16, 16), ("o256", 0, 256, 1), ("fb", 0, 2, 0), ("fb", 272, 288, 1),
-                          ("fc", 0, 2, 0), ("fc", 176, 192, 1), ("cm", 0, 2, 0)):
+    for name, a, b, v in (("c16", 0, 16, 16), ("fb", 0, 2, 0), ("fb", 272, 288, 1), ("cm", 0, 2, 0)):
         iota(R(name, a, b), [[0, b - a]], v, 0, True)
     iota(R("cow", 1280, 2240), [[0, 960]], 2048, 0, False)
     iota(R("sw", 0, 1536), [[0, 1536]], 0, 0, True)
@@ -220,19 +234,12 @@ def rank_program(g, core, T, topo):
     dma("y", R("cow", 0, 1280), T.co[:, 512:1792])
 
     def later_constants():
-        ts(R("pe1"), R("qm"), 0.0, A.is_equal)
-        ts(R("pe2", 16, 128), R("qm", 16, 128), 16.0, A.is_equal)
-        ts(R("pe2", 0, 16), R("pm", 0, 16), 0.0, A.is_equal)
         ts(R("wn", 0, 1792), R("yv", 0, 1792), 0.25, A.mult)
         ms(R("mx", 0, 1024, 16), 0.0)
-        cp(R("mof"), R("moi"))
-        ts(R("nid"), R("pm"), 0.0, A.is_equal, -1.0, A.mult)
         ms(R("mn", 0, 1024, 16), 1e20)
+        cp(R("mof"), R("moi"))
         ts(R("qt"), R("ki"), -1.0 / 256, A.mult)
-        ts(R("trt"), R("pm"), 0.0, A.is_le)
-        ts(R("one"), R("mg"), fcol(0), A.is_equal)
         ts(fcol(7), fcol(1), 2304.0, A.add)
-        tt(R("tri"), R("one"), R("trt"), A.mult)
         dma("y", R("mob", 0, 1280, part=slice(0, 128, 16)), R("mof"))
 
     def cells_a(fb, n, spare, high):
@@ -257,6 +264,7 @@ def rank_program(g, core, T, topo):
         scan(R("ff"), R("o256"), R("sw", a, a + 256), A.add, A.max)
         wrap(R("ps1", 0, 16), "ff", 0, 256)
 
+    banks = ("ps0", "ps2", "ps3", "ps6", "ps1")
     left = {"v": [], "s": []}
 
     def rows(nv, ns):
@@ -282,12 +290,13 @@ def rank_program(g, core, T, topo):
             release_values(t - 1)
             ts(R("fb", 144, 272), R("ps0", 0, 128), -8.0, A.is_lt)
             cells_a("fb", 144, R("pt2", 6, 22), True)
-            cells_b(144, 2 * t - 1)
-            ts(R("tl", 0, 16), R("ps1", 0, 16), 1.0 / 32, A.mult, -2048.0, A.add)
-            ts(R("tl", 16, 17), R("ps1", 0, 1), 1.0 / 32, A.mult, -2048.0, A.add)
-            cp(R("pd"), IND(R("prw", lo, WW), tl))
             turn("ps6", "lg", t)
             act(R("yv", 2048, 2240), R("ps6", 0, 192), F.Identity, bias=-1.0)
+            act(R("wn", 2048, 2240), R("ps6", 0, 192), F.Identity, scale=0.25, bias=-0.25)
+            cells_b(144, 2 * t - 1)
+            ts(R("tl", 0, 16), R("ps1", 0, 16), 1.0 / 32, A.mult, -2048.0, A.add)
+            cp(R("pd"), IND(R("prw", lo, WW), tl))
+            ts(R("tl", 16, 17), R("ps1", 0, 1), 1.0 / 32, A.mult, -2048.0, A.add)
         cp(R("gp"), IND(R("prw", lo, WW), R("tl", 0, 17)))
         tr(R("tt", 0, 256), R("gp", 0, 256))
         tr(R("tt", 256, 512), R("gp", 16, 272))
@@ -298,7 +307,8 @@ def rank_program(g, core, T, topo):
             later_constants()
             turn("ps6", "lg", t)
             act(R("yv", 2048, 2240), R("ps6", 0, 192), F.Identity, bias=-1.0)
-        act(R("wn", 2048, 2240), R("ps6", 0, 192), F.Identity, scale=0.25, bias=-0.25)
+            act(R("wn", 2048, 2240), R("ps6", 0, 192), F.Identity, scale=0.25, bias=-0.25)
+        act(R("otl"), IND(R("yv", lo, WW), tl), F.Copy)
         for c in range(4):
             a = 1024 * c
             if c < VG:
@@ -307,9 +317,9 @@ def rank_program(g, core, T, topo):
                 act(R("vb", a, a + 1024), IND(R("yv"), R("pd", 64 * c, 64 * c + 64)), F.Copy)
             scan(R("smn", a, a + 1024), R("mn", 0, 1024), R("vb", a, a + 1024), A.add, A.min)
             if c == 3:
-                act(R("otl"), IND(R("yv", lo, WW), tl), F.Copy)
                 rows(0, S0)
                 act(R("rr"), R("smn", 15, 4096, 16), F.Relu, scale=-64.0)
+                rows(0, S0)
             scan(R("smx", a, a + 1024), R("mx"), R("vb", a, a + 1024), A.mult, A.max)
         p3 = R("ps3", 0, 256)
         mm([(p3, R("nid"), R("smn", 15, 4096, 16)), (p3, R("nid"), R("otl")), (p3, R("nid"), R("rr")),
@@ -339,8 +349,9 @@ def rank_program(g, core, T, topo):
         rl = R("rl")
         cp(R("pu"), IND(R("prw", 512, WW), rl))
         rows(0, 16)
+        for j in range(MB):
+            mm([(R(banks[j], 0, 448), R("id32"), R("mk", 448 * j, 448 * j + 448))])
         act(R("junk"), R("ps7", 0, 128), F.Identity, scale=2.0, accum=R("ec"))
-        act(R("ebc"), R("o256"), F.Relu, scale=R("ec"))
         act(R("orl"), IND(R("yv", 512, WW), rl), F.Copy)
         act(R("mog"), IND(R("mob"), rl), F.Copy)
         act(R("pa"), R("orl"), F.Identity, bias=256.5)
@@ -357,7 +368,12 @@ def rank_program(g, core, T, topo):
             mm([(o, R("idm"), R("dg", a + k, a + 1024, 16)) for k in range(16)]
                + [(o, R(m), R(x, 64 * c, 64 * c + 64)) for m, x in (("one", "mog"), ("idm", "pa"), ("nid", "orl"))])
         rows(16, 0)
-        tt(R("wn", 0, 2240), R("wn", 0, 2240), R("mk", 0, 2240), A.mult)
+        if MB < 5:
+            tt(R("wn", 448 * MB, 2240), R("wn", 448 * MB, 2240), R("mk", 448 * MB, 2240), A.mult)
+        for j in range(MB):
+            a = 448 * j
+            tt(R("wn", a, a + 448), R(banks[j], 0, 448), R("wn", a, a + 448), A.mult)
+        ts(R("ebc"), R("o256"), R("ec"), A.mult, 0.0, A.max)
         ts(R("sn", 192 * t, 192 * t + 192), R("wn", 2048, 2240), -0.5, A.is_lt, 7.0, A.mult)
         exchange("sn", "ln", t, "a%d" % (4 + t))
         if t < 3:

import numpy as np
from concourse.bass import DstId, RemoteDMATransfer
from concourse.mybir import AluOpType, ActivationFunctionType

N = 4
WW = 2752
VG, VD, HV = 1, 1, 2
NS, S0, S1, S2 = 10, 1, 3, 4
MB = 2
NS0, SE = 10, 1
B16, F32, I32, U16 = "bfloat16", "float32", "int32", "uint16"
SB = {
    "yv": (WW, B16), "wn": (WW, B16), "mk": (WW, F32), "prw": (WW, I32), "cow": (2240, I32), "mob": (2240, B16),
    "moi": (80, I32), "mof": (80, B16), "bdi": (12, I32), "bdu": (12, U16),
    "sw": (3984, F32), "mx": (1024, B16), "mn": (1024, B16), "c8": (256, F32), "id32": (128, F32),
    "vb": (4096, B16), "smx": (4096, B16), "smn": (4096, B16), "dg": (4096, B16),
    "hv": (4096, B16), "hm": (3072, B16),
    "oy": (2048, B16), "of": (2048, B16), "ow": (2048, B16),
    "sg": (768, B16), "lg": (768, B16), "sn": (768, B16), "ln": (768, B16),
    "pc": (8, I32), "fc0": (16, F32), "pm": (128, F32), "qm": (128, F32), "mg": (128, F32), "ki": (16, F32),
    "idm": (128, B16), "nid": (128, B16), "one": (128, B16), "tri": (128, B16), "trt": (128, B16),
    "pe1": (128, B16), "pe2": (128, B16), "bsel": (144, B16),
    "t16": (16, B16), "qt": (16, B16), "c16": (16, B16), "sl": (16, U16), "pt1": (128, B16), "pt2": (40, B16),
    "o256": (256, B16), "fb": (288, B16), "fc": (192, B16), "dv": (144, F32), "tc": (16, F32), "tb": (16, F32),
    "off": (10, U16), "ff": (256, B16), "tl": (18, U16), "rl": (16, U16), "w1": (16, F32), "w2": (16, F32),
    "gp": (272, F32), "tt": (512, F32), "ptt": (256, U16), "pd": (256, U16), "pu": (256, U16), "cu": (256, U16),
    "otl": (256, B16), "rr": (256, B16), "yn": (256, B16), "sgn": (128, B16), "junk": (128, B16), "ec": (1, F32),
    "ebc": (256, B16), "orl": (256, B16), "pa": (256, B16),
    "mog": (256, B16), "fs": (256, B16), "am": (256, B16), "gy": (192, B16), "ga": (192, B16), "nw": (256, B16),
    "fr": (256, B16), "cm": (258, B16), "go": (256, B16), "m1": (256, B16), "nt": (192, B16), "nu": (192, B16),
    "m0": (256, B16),
}
SCRATCH = {k: ("sbuf", [128, v[0]], v[1]) for k, v in SB.items()}
for _i in range(8):
    SCRATCH["ps%d" % _i] = ("psum", [128, 512], F32)
NDMA = 16
SEMAPHORES = ["qv", "qs", "qp", "qg", "sent"] + ["d%d" % i for i in range(NDMA)] + ["a%d" % i for i in range(8)]


def rank_program(g, core, T, topo):
    rank = T.rank_of(core)
    if rank is None:
        return
    A = AluOpType
    F = ActivationFunctionType
    Q = {"v": g.vector, "s": g.scalar, "p": g.tensor, "g": g, "y": g.sync}
    ops = []
    nd = [0]

    def R(name, a=None, b=None, s=None, part=None):
        t = T[name]
        m = np.zeros(t.shape[1], bool)
        sl = slice(a, b, s)
        m[sl] = True
        if name.startswith("ps"):
            m[:] = True
        ap = t[:, sl] if part is None else t[part, sl]
        return (ap, [(name, m)])

    def IND(win, off):
        return (win[0].indirect(off[0]), win[1], off[1])

    def acc(xs):
        out = []
        for x in xs:
            if isinstance(x, tuple):
                out += x[1]
                if len(x) == 3:
                    out += x[2]
        return out

    def ap(x):
        return x[0] if isinstance(x, tuple) else x

    def put(q, emit, ins, out):
        rd = acc(ins)
        wr = []
        for o in out:
            wr += o[1]
            if len(o) == 3:
                rd += o[2]
        ops.append((q, emit, rd, wr, None, 0))

    def cp(o, i):
        put("v", lambda: g.vector.tensor_copy(o[0], i[0]), [i], [o])

    def tt(o, a, b, op):
        put("v", lambda: g.vector.tensor_tensor(o[0], a[0], b[0], op), [a, b], [o])

    def ts(o, a, s1, op0, s2=None, op1=None):
        if op1 is None:
            put("v", lambda: g.vector.tensor_scalar(o[0], a[0], ap(s1), None, op0), [a, s1], [o])
        else:
            put("v", lambda: g.vector.tensor_scalar(o[0], a[0], ap(s1), ap(s2), op0, op1), [a, s1, s2], [o])

    def scan(o, d0, d1, op0, op1):
        put("v", lambda: g.vector.tensor_tensor_scan(o[0], d0[0], d1[0], 0.0, op0, op1), [d0, d1], [o])

    def ms(o, c):
        put("v", lambda: g.vector.memset(o[0], c), [], [o])

    def tr(o, i):
        put("v", lambda: g.vector.transpose(o[0], i[0]), [i], [o])

    def act(o, i, f, scale=1.0, bias=0.0, accum=None):
        if len(o) == 3:
            put("s", lambda: g.scalar.activation(o[0], i[0], f), [i], [o])
        elif accum is None:
            put("s", lambda: g.scalar.activation(o[0], i[0], f, bias=bias, scale=ap(scale)), [i, scale], [o])
        else:
            put("s", lambda: g.scalar.activation(o[0], i[0], f, bias=bias, scale=scale, accum_out=accum[0]),
                [i], [o, accum])

    def mm(terms):
        def emit():
            h = None
            for n, (o, l, r) in enumerate(terms):
                h = g.tensor.matmul(o[0], l[0], r[0], n == 0, n == len(terms) - 1)
            return h
        put("p", emit, [x[1] for x in terms] + [x[2] for x in terms], [terms[0][0]])

    def iota(o, pat, base, cm_, flt):
        if flt:
            put("g", lambda: g.iota(o[0], pat, base, cm_, allow_small_or_imprecise_dtypes=True), [], [o])
        else:
            put("g", lambda: g.iota(o[0], pat, base, cm_), [], [o])

    def asel(o, i, pat, op, base, cm_):
        put("g", lambda: g.affine_select(o[0], i[0], pat, op, 0.0, base, cm_), [i], [o])

    def dma(q, o, i, after=()):
        s = "d%d" % nd[0]
        nd[0] += 1
        ops.append((q, lambda: Q[q].dma_start(ap(o), ap(i)), acc([i]) + acc(after), acc([o]), s, 16))

    nsent = [0]

    def exchange(src, dst, slot, sem):
        trs = []
        tot = 0
        for d in range(1, N):
            peer = T.cores[rank ^ d]
            rid, pid, _ = topo.addr(peer)
            eng = topo.engines(core, peer)
            per = len(eng) // N
            mask = sum(1 << e for e in eng[per * (d - 1):per * d])
            tot += len(topo.engines(peer, core)) // N
            nsent[0] += per
            a = 192 * slot + 64 * (d - 1)
            trs.append(RemoteDMATransfer(dst_ids=[DstId(rid=rid, pnc=pid)], dma_engine_mask=mask,
                                         remote_sem=T.sem[sem], src=T[src][:, a:a + 64], dst=T[dst][:, a:a + 64]))
        ops.append(("g", lambda: g.remote_dma_fused(trs, local_sem=T.sem.sent),
                    acc([R(src, 192 * slot, 192 * slot + 192)]), [], "-", 0))
        ops.append(("x", None, [], acc([R(dst, 192 * slot, 192 * slot + 192)]), sem, tot))

    def sel(x):
        return R("bsel", 15 - x, 143 - x)

    def wrap(out, name, a, b, more=()):
        mm([(out, sel(x), R(name, a + x, b, 16)) for x in range(16)] + list(more))

    def turn(ps, name, slot):
        for d, m in enumerate(("pe1", "pe2", "idm")):
            a = 192 * slot + 64 * d
            mm([(R(ps, 64 * d, 64 * d + 64), R(m), R(name, a, a + 64))])

    def pc(i):
        return R("pc", i, i + 1)

    def fcol(i):
        return R("fc0", i, i + 1)

    dma("y", R("wn", 1792, 2048), T.y0[:, 1792:2048])
    dma("y", R("yv", 0, 2048), T.y0[:])
    dma("s", R("prw", 1792, 2048), T.pr[:, 1792:2048])
    dma("s", R("bdi"), T.bd[:])
    dma("y", R("moi"), T.mo[:, 512:1792])
    iota(pc(0), [[0, 1]], 0, 1, False)
    iota(R("ki"), [[1, 16]], 0, 0, True)
    iota(R("pm"), [[-1, 128]], 0, 1, True)
    iota(R("prw", 2048, WW), [[1, WW - 2048]], 2048, 0, False)
    ms(R("mx"), 1.0)
    asel(R("pe1"), R("mx", 0, 128), [[16, 8], [-1, 16]], A.is_equal, -112, 1)
    asel(R("pe2", 16, 128), R("mx", 0, 112), [[16, 7], [-1, 16]], A.is_equal, -112, 1)
    asel(R("pe2", 0, 16), R("mx", 0, 16), [[-1, 16]], A.is_equal, 0, 1)
    for a in range(0, WW, 1024):
        act(R("mk", a, min(a + 1024, WW)), R("mx", 0, min(1024, WW - a)), F.Copy)
    ms(R("bsel"), 0.0)
    ts(pc(1), pc(0), 4, A.arith_shift_right)
    ts(pc(2), pc(0), 15, A.bitwise_and)
    ms(R("c8"), 8.0)
    tt(pc(3), pc(0), pc(1), A.add)
    cp(fcol(0), pc(1))
    cp(fcol(1), pc(2))
    ts(pc(4), pc(3), 1, A.bitwise_and)
    ts(R("idm"), R("pm"), 0.0, A.is_equal)
    ts(R("bsel", 15, 143, 16), R("ki", 0, 8), fcol(0), A.is_equal)
    ts(fcol(3), fcol(1), 0.0, A.is_equal, 256.0, A.mult)
    cp(fcol(2), pc(4))
    ts(R("t16"), R("ki"), 16.0, A.mult)
    ts(fcol(6), fcol(1), 448.0, A.add)
    ts(R("m0"), R("wn", 1792, 2048), 0.0, A.min, 28.0, A.mult)
    wrap(R("ps1", 0, 16), "m0", 0, 256, [(R("ps1", 0, 16), R("idm"), R("t16"))])
    ts(fcol(4), fcol(3), 240.0, A.add, fcol(2), A.mult)
    cp(R("bdu"), R("bdi"))
    ts(fcol(5), fcol(1), 16.0, A.mult, fcol(4), A.add)
    ms(R("yv", 2240, WW), 0.0)
    ts(R("sl"), R("ki"), fcol(5), A.add)
    act(R("sg", 0, 192), IND(R("yv", 0, 2048), R("bdu")), F.Relu, bias=1.0)
    exchange("sg", "lg", 0, "a0")
    act(R("mn"), R("mx"), F.Copy, scale=0.0)
    iota(R("wn", 2240, WW), [[0, WW - 2240]], 0, 0, True)
    iota(R("nid"), [[0, 128]], -1, 0, True)
    asel(R("nid"), R("nid"), [[-1, 128]], A.is_equal, 0, 1)
    iota(R("one"), [[0, 128]], 1, 0, True)
    asel(R("one"), R("one"), [[-16, 8], [0, 16]], A.is_ge, 0, 1)
    asel(R("one"), R("one"), [[16, 8], [0, 16]], A.is_ge, 15, -1)
    asel(R("tri"), R("one"), [[1, 128]], A.is_ge, 0, -1)
    iota(R("id32"), [[0, 128]], 1, 0, True)
    asel(R("id32"), R("id32"), [[-1, 128]], A.is_equal, 0, 1)
    iota(R("pt1"), [[32, 128]], 4096, 0, True)
    iota(R("pt2"), [[64, 40]], 8192, 0, True)
    iota(R("sw", 1536, 1792), [[0, 256]], 0, 0, True)
    ts(R("tl", 0, 16), R("ps1", 0, 16), fcol(6), A.add)
    ts(R("tl", 16, 17), R("ps1", 0, 1), fcol(6), A.add)
    for name, a, b, v in (("fc", 0, 2, 0), ("fc", 176, 192, 1), ("o256", 0, 256, 1)):
        iota(R(name, a, b), [[0, b - a]], v, 0, True)
    iota(R("mob"), [[0, 2240]], 0, 0, True)
    for name, a, b, v in (("c16", 0, 16, 16), ("fb", 0, 2, 0), ("fb", 272, 288, 1), ("cm", 0, 2, 0)):
        iota(R(name, a, b), [[0, b - a]], v, 0, True)
    iota(R("cow", 1280, 2240), [[0, 960]], 2048, 0, False)
    iota(R("sw", 0, 1536), [[0, 1536]], 0, 0, True)
    dma("y", R("prw", 0, 1792), T.pr[:, 0:1792], after=[R("lg", 0, 192)])
    dma("y", R("cow", 0, 1280), T.co[:, 512:1792])

    def later_constants():
        ts(R("wn", 0, 1792), R("yv", 0, 1792), 0.25, A.mult)
        ms(R("mx", 0, 1024, 16), 0.0)
        ms(R("mn", 0, 1024, 16), 1e20)
        cp(R("mof"), R("moi"))
        ts(R("qt"), R("ki"), -1.0 / 256, A.mult)
        ts(fcol(7), fcol(1), 2304.0, A.add)
        dma("y", R("mob", 0, 1280, part=slice(0, 128, 16)), R("mof"))

    def cells_a(fb, n, spare, high):
        r = n - 16
        t = [(R("ps2", 0, n), R("tri"), R(fb, n, 2 * n)), (R("ps2", 0, r), R("nid"), R("pt1", 0, r)),
             (R("ps2", r, n), R("nid"), spare)]
        if high:
            t.append((R("ps2", r, n), R("nid"), R("c16")))
        scan(R(fb, 1, n), R(fb, n, 2 * n - 1), R(fb, n, 2 * n - 1), A.add, A.max)
        mm(t)
        act(R("dv", 0, n), R("ps2", 0, n), F.Identity, scale=-1.0, bias=16.5)
        q = n // 16
        wrap(R("ps1", 0, 2 * q), fb, 0, 2 * n, [(R("ps1", q, 2 * q), R("idm"), R("qt", 0, q))])

    def cells_b(n, use):
        q = n // 16
        a = 256 * (6 - use)
        ts(R("tc", 0, q), R("ps1", q, 2 * q), -4096.0, A.mult, fcol(7), A.add)
        tt(R("tb", 0, q), R("ps1", 0, q), R("tc", 0, q), A.max)
        cp(R("off", 0, q), R("tb", 0, q))
        cp(IND(R("sw", a, a + 2448), R("off", 0, q)), R("dv", 0, n))
        scan(R("ff"), R("o256"), R("sw", a, a + 256), A.add, A.max)
        wrap(R("ps1", 0, 16), "ff", 0, 256)

    banks = ("ps0", "ps2", "ps3", "ps6", "ps1")
    left = {"v": [], "s": []}

    def rows(nv, ns):
        for _ in range(min(nv, len(left["v"]))):
            k = left["v"].pop(0)
            cp(IND(R("wn"), R("ptt", 16 * k, 16 * k + 16)), R("vb", k, 4096, 16))
        for _ in range(min(ns, len(left["s"]))):
            k = left["s"].pop(0)
            act(IND(R("mk"), R("ptt", 16 * k, 16 * k + 16)), R("c8"), F.Silu)

    def release_values(t):
        tt(R("m1"), R("go"), R("am"), A.mult)
        tt(IND(R("yv", 512, WW), R("rl")), R("orl"), R("m1"), A.add)

    for t in range(4):
        lo = 1792 if t == 0 else 0
        tl = R("tl", 0, 16)
        ns = NS0 if t == 0 else NS
        left["v"] = list(range(16 - ns))
        left["s"] = list(range(16 - ns, 16))
        if t > 0:
            wrap(R("ps0", 0, 128), "wn", 0, 2048)
            release_values(t - 1)
            ts(R("fb", 144, 272), R("ps0", 0, 128), -8.0, A.is_lt)
            cells_a("fb", 144, R("pt2", 6, 22), True)
            turn("ps6", "lg", t)
            act(R("yv", 2048, 2240), R("ps6", 0, 192), F.Identity, bias=-1.0)
            act(R("wn", 2048, 2240), R("ps6", 0, 192), F.Identity, scale=0.25, bias=-0.25)
            cells_b(144, 2 * t - 1)
            ts(R("tl", 0, 16), R("ps1", 0, 16), 1.0 / 32, A.mult, -2048.0, A.add)
            cp(R("pd"), IND(R("prw", lo, WW), tl))
            ts(R("tl", 16, 17), R("ps1", 0, 1), 1.0 / 32, A.mult, -2048.0, A.add)
        cp(R("gp"), IND(R("prw", lo, WW), R("tl", 0, 17)))
        tr(R("tt", 0, 256), R("gp", 0, 256))
        tr(R("tt", 256, 512), R("gp", 16, 272))
        cp(R("ptt"), IND(R("tt"), R("sl")))
        if t == 0:
            rows(0, SE)
            cp(R("pd"), R("gp", 0, 256))
            later_constants()
            turn("ps6", "lg", t)
            act(R("yv", 2048, 2240), R("ps6", 0, 192), F.Identity, bias=-1.0)
            act(R("wn", 2048, 2240), R("ps6", 0, 192), F.Identity, scale=0.25, bias=-0.25)
        act(R("otl"), IND(R("yv", lo, WW), tl), F.Copy)
        for c in range(4):
            a = 1024 * c
            if c < VG:
                cp(R("vb", a, a + 1024), IND(R("yv"), R("pd", 64 * c, 64 * c + 64)))
            else:
                act(R("vb", a, a + 1024), IND(R("yv"), R("pd", 64 * c, 64 * c + 64)), F.Copy)
            scan(R("smn", a, a + 1024), R("mn", 0, 1024), R("vb", a, a + 1024), A.add, A.min)
            if c == 3:
                rows(0, S0)
                act(R("rr"), R("smn", 15, 4096, 16), F.Relu, scale=-64.0)
                rows(0, S0)
            scan(R("smx", a, a + 1024), R("mx"), R("vb", a, a + 1024), A.mult, A.max)
        p3 = R("ps3", 0, 256)
        mm([(p3, R("nid"), R("smn", 15, 4096, 16)), (p3, R("nid"), R("otl")), (p3, R("nid"), R("rr")),
            (p3, R("idm"), R("smx", 15, 4096, 16))])
        act(R("yn"), p3, F.Relu)
        rows(1, 0)
        tt(IND(R("yv", lo, WW), tl), R("yn"), R("otl"), A.add)
        wrap(R("ps0", 0, 128), "yv", 0, 2048)
        rows(2, S1)
        c0 = 26 * t
        ts(R("fc", 96, 176 - c0), R("ps0", 32 + c0, 112), 0.0, A.is_ge)
        if c0:
            ts(R("fc", 176 - c0, 176), R("ps0", 32, 32 + c0), 0.0, A.is_ge)
        spare = (R("pt1", 108, 124), R("pt2", 17, 33), R("pt2", 4, 20), R("pt1", 110, 126))[t]
        cells_a("fc", 96, spare, t in (1, 2))
        act(R("sgn"), R("ps0", 0, 128), F.Sign, bias=0.5)
        rows(1, S2)
        cells_b(96, 2 * t)
        mm([(R("ps7", 0, 128), R("one"), R("sgn"))])
        rows(1, 0)
        if t == 0:
            ts(R("rl"), R("ps1", 0, 16), 1.0 / 32, A.mult, -2048.0, A.add)
        else:
            ts(R("w1"), R("ps1", 0, 16), 32.0 * (2048 + 1280 - 416 * t), A.is_ge, -32.0 * 1280, A.mult)
            tt(R("w2"), R("ps1", 0, 16), R("w1"), A.add)
            ts(R("rl"), R("w2"), 1.0 / 32, A.mult, 416.0 * t - 2048.0, A.add)
        rl = R("rl")
        cp(R("pu"), IND(R("prw", 512, WW), rl))
        rows(0, 16)
        for j in range(MB):
            mm([(R(banks[j], 0, 448), R("id32"), R("mk", 448 * j, 448 * j + 448))])
        act(R("junk"), R("ps7", 0, 128), F.Identity, scale=2.0, accum=R("ec"))
        act(R("orl"), IND(R("yv", 512, WW), rl), F.Copy)
        act(R("mog"), IND(R("mob"), rl), F.Copy)
        act(R("pa"), R("orl"), F.Identity, bias=256.5)
        cp(R("cu"), IND(R("cow"), rl))
        for c in range(4):
            a = 1024 * c
            lst = IND(R("yv"), R("pu", 64 * c, 64 * c + 64))
            if c >= 4 - VD:
                rows(16, 0)
                ts(R("dg", a, a + 1024), lst, 0.0, A.min, -1.0 / 64, A.mult)
            else:
                act(R("dg", a, a + 1024), lst, F.Relu, scale=-1.0 / 64)
            o = R("ps4", 64 * c, 64 * c + 64)
            mm([(o, R("idm"), R("dg", a + k, a + 1024, 16)) for k in range(16)]
               + [(o, R(m), R(x, 64 * c, 64 * c + 64)) for m, x in (("one", "mog"), ("idm", "pa"), ("nid", "orl"))])
        rows(16, 0)
        if MB < 5:
            tt(R("wn", 448 * MB, 2240), R("wn", 448 * MB, 2240), R("mk", 448 * MB, 2240), A.mult)
        for j in range(MB):
            a = 448 * j
            tt(R("wn", a, a + 448), R(banks[j], 0, 448), R("wn", a, a + 448), A.mult)
        ts(R("ebc"), R("o256"), R("ec"), A.mult, 0.0, A.max)
        ts(R("sn", 192 * t, 192 * t + 192), R("wn", 2048, 2240), -0.5, A.is_lt, 7.0, A.mult)
        exchange("sn", "ln", t, "a%d" % (4 + t))
        if t < 3:
            iota(R("mk", 0, 2240), [[0, 2240]], 1, 0, True)
        ms(R("wn", 2048, 2240), 0.0)
        tt(IND(R("wn", lo, WW), tl), R("yn"), R("otl"), A.add)
        for c in range(4):
            a = 1024 * c
            lst = IND(R("wn", 0, 2064), R("cu", 64 * c, 64 * c + 64))
            if c < HV:
                cp(R("hv", a, a + 1024), lst)
                scan(R("hm", a, a + 1024), R("mn"), R("hv", a, a + 1024), A.add, A.min)
                continue
            act(R("hv", a, a + 1024), lst, F.Relu, scale=-1.0, bias=-0.5)
            if c == HV:
                act(R("fs"), R("ps4", 0, 256), F.Sign, bias=-258.0 - 1.0 / 128)
            o = R("ps5", 64 * c, 64 * c + 64)
            mm([(o, R("idm"), R("hv", a + k, a + 1024, 16)) for k in range(16)])
            if c == HV:
                mm([(p3, R("one"), R("fs"))])
        act(R("nw"), p3, F.Square, scale=3.75 ** 0.5 / 16)
        act(R("fr", 64 * HV, 256), R("ps5", 64 * HV, 256), F.Relu, scale=-8.0, bias=4.0)
        p4 = R("ps4", 0, 256)
        mm([(p4, R("idm"), R("orl")), (p4, R("idm"), R("orl")), (p4, R("idm"), R("fs"))])
        turn("ps7", "ln", t)
        if t < 3:
            act(R("gy"), IND(R("yv", 0, 2048), R("bdu")), F.Copy)
        act(R("am"), p4, F.Identity, scale=0.125, bias=0.375)
        act(R("nt"), R("ps7", 0, 192), F.Identity, bias=1.0)
        ts(R("fr", 0, 64 * HV), R("hm", 15, 1024 * HV, 16), -0.5, A.is_ge, 4.0, A.mult)
        scan(R("cm", 2, 258), R("fr"), R("ebc"), A.add, A.min)
        tt(R("go"), R("cm", 1, 257), R("cm", 2, 258), A.subtract)
        if t == 3:
            release_values(t)
            for h in range(2):
                a = 1024 * h
                ts(R("oy", a, a + 1024), R("yv", a, a + 1024), -1.0, A.max)
                dma("y", T.yy[:, a:a + 1024], R("oy", a, a + 1024))
                act(R("of", a, a + 1024), R("yv", a, a + 1024), F.Relu, scale=-1.0, bias=-1.0)
                dma("s", T.yf[:, a:a + 1024], R("of", a, a + 1024))
        tt(IND(R("wn", 512, WW), rl), R("go"), R("nw"), A.add)
        if t < 3:
            act(R("ga"), IND(R("wn", 0, 2048), R("bdu")), F.Relu, scale=-128.0)
            p6 = R("ps6", 0, 192)
            mm([(p6, R("idm"), R("gy")), (p6, R("nid"), R("ga"))])
            act(R("sg", 192 * t + 192, 192 * t + 384), p6, F.Relu, bias=1.0)
            exchange("sg", "lg", t + 1, "a%d" % (t + 1))
        tt(R("nu"), IND(R("wn", 0, 2048), R("bdu")), R("nt"), A.mult)
        cp(IND(R("wn", 0, 2048), R("bdu")), R("nu"))
    ts(R("ow"), R("wn", 0, 2048), -0.5, A.is_lt)
    dma("y", T.yw[:], R("ow", part=slice(0, 128, 16)))

    hist = {}
    deps = []
    for n, (q, emit, rd, wr, sem, cnt) in enumerate(ops):
        d = set()
        for kind, lst in ((0, rd), (1, wr)):
            for name, m in lst:
                bank = name.startswith("ps")
                for (j, mj, kj) in hist.get(name, []):
                    if j == n or not (kind or kj or bank) or not (m & mj).any():
                        continue
                    if ops[j][0] == q and ops[j][4] is None and sem is None and (q == "p" or not (kind or kj)):
                        continue
                    d.add(j)
        for kind, lst in ((0, rd), (1, wr)):
            for name, m in lst:
                hist.setdefault(name, []).append((n, m, kind))
        last = {}
        for j in d:
            key = ops[j][4] or ops[j][0]
            last[key] = max(last.get(key, -1), j)
        deps.append(last)
    seen = {q: {} for q in Q}
    need = []
    marked = set()
    for n, op in enumerate(ops):
        w = []
        if op[0] != "x":
            for key, j in deps[n].items():
                if seen[op[0]].get(key, -1) < j:
                    seen[op[0]][key] = j
                    w.append(j)
                    marked.add(j)
        need.append(w)
    count = {q: 0 for q in Q}
    val = {}
    for n, (q, emit, rd, wr, sem, cnt) in enumerate(ops):
        if sem is None:
            if n in marked:
                count[q] += 1
                val[n] = ("q" + q, count[q])
        else:
            val[n] = (sem, cnt)
    for n, (q, emit, rd, wr, sem, cnt) in enumerate(ops):
        if q == "x":
            continue
        for j in need[n]:
            Q[q].wait_ge(T.sem[val[j][0]], val[j][1])
        h = emit()
        if sem is None:
            if n in marked:
                h.then_inc(T.sem["q" + q], 1)
        elif sem != "-":
            h.then_inc(T.sem[sem], 16)
    for n, op in enumerate(ops):
        if op[4] not in (None, "-") and n not in marked:
            g.sync.wait_ge(T.sem[op[4]], op[5])
    g.wait_ge(T.sem.sent, nsent[0])
